import numpy as np
import ml_dtypes


def mxq(x, axis, fmt="e4m3"):
    dtype, down = {"e4m3": (ml_dtypes.float8_e4m3fn, 7), "e5m2": (ml_dtypes.float8_e5m2, 14)}[fmt]
    v = np.moveaxis(np.asarray(x, np.float32).astype(ml_dtypes.bfloat16).astype(np.float64), axis, -1)
    blocks = v.reshape(v.shape[:-1] + (-1, 32))
    amax = np.abs(blocks).max(-1, keepdims=True)
    byte = np.maximum(np.where(amax > 0, np.frexp(amax)[1] - 1 + 127, 0) - down, 1)
    scale = np.exp2(byte - 127.0)
    codes = (blocks / scale).astype(np.float32).astype(dtype).astype(np.float64)
    return np.moveaxis((codes * scale).reshape(v.shape), -1, axis)


WIDE = False


def mx_kscale(k):
    if not WIDE:
        return np.ones(k)
    levels = np.array([10, -10, 5, -5, 0])
    if k % 512:
        return np.exp2(np.random.permutation(np.resize(levels, k // 32))).repeat(32)
    a = np.empty((k // 512, 16))
    for p in range(k // 512):
        a[p, :8] = np.random.permutation(np.resize(levels, 8))
        for g in range(8):
            far = levels[np.abs(levels - a[p, g]) >= 10]
            a[p, g + 8] = far[np.random.randint(len(far))]
    return np.exp2(a.ravel()).repeat(32)


def f64(x):
    return np.asarray(x).astype(np.float64)


def striped(idx):
    return np.tile(np.asarray(idx).reshape(-1, 16).T, (8, 1)).astype(np.uint16)


def unstriped(offs):
    return offs[:16].T.reshape(-1).astype(np.int64)


E2M1 = np.array([0.0, 0.5, 1.0, 1.5, 2.0, 3.0, 4.0, 6.0, -0.0, -0.5, -1.0, -1.5, -2.0, -3.0, -4.0, -6.0])


def pack_weight(w, fmt):
    k, n = w.shape
    w = f64(np.asarray(w, np.float32).astype(ml_dtypes.bfloat16)).reshape(k // 32, 32, n)
    amax = np.abs(w).max(1)
    if fmt == "e4m3":
        byte = np.frexp(amax)[1] - 1 + 127 - 7
    else:
        mant, ex = np.frexp(amax / 6.0)
        byte = np.where(mant > 0.5, ex, ex - 1) + 127
    byte = np.clip(np.where(amax > 0, byte, 1), 1, 254)
    scaled = (w * np.exp2(127.0 - byte)[:, None, :]).reshape(k, n).astype(np.float32)
    by_word = np.ascontiguousarray(scaled.reshape(k // 512, 128, 4, n).transpose(0, 1, 3, 2))
    if fmt == "e4m3":
        words = by_word.astype(ml_dtypes.float8_e4m3fn).view(np.uint8)
    else:
        c = by_word.astype(ml_dtypes.float4_e2m1fn).view(np.uint8) & 0xF
        words = (c[..., 0::2] | (c[..., 1::2] << 4)).reshape(k // 512, 128, 2 * n)
    return np.ascontiguousarray(words), np.ascontiguousarray(byte.astype(np.uint8).reshape(k // 512, 16, n))


def unpack_weight(words, scales, fmt):
    g, _, n = scales.shape
    words = np.ascontiguousarray(words).reshape(g, 128, n, -1)
    if fmt == "e4m3":
        vals = words.view(ml_dtypes.float8_e4m3fn).astype(np.float64)
    else:
        nib = np.empty((g, 128, n, 4), np.uint8)
        nib[..., 0::2] = words & 0xF
        nib[..., 1::2] = words >> 4
        vals = E2M1[nib]
    vals = vals * np.repeat(np.exp2(scales.astype(np.float64) - 127.0), 8, axis=1)[..., None]
    return vals.transpose(0, 1, 3, 2).reshape(g * 512, n)


def sigmoid(v):
    return 1.0 / (1.0 + np.exp(-v))


D, E, T, I, Q = 512, 512, 2048, 512, 128


def setup_inputs():
    n = np.random.standard_normal
    idx = np.random.permutation(T)[:I]
    fd = mx_kscale(D)
    fe = mx_kscale(E)
    keysp = pack_weight(n((D, T)) / fd[:, None], "e4m3")
    valsp = pack_weight(n((E, T)) / fe[:, None], "e4m3")
    return {
        "query": (n((D, Q)) * 1.0 / np.sqrt(D) * fd[:, None]).astype(np.float32),
        "query2": (n((D, Q)) * 1.0 / np.sqrt(D) * fd[:, None]).astype(np.float32),
        "keys_words": keysp[0],
        "keys_scales": keysp[1],
        "th": (np.random.uniform(0.3, 1.5, (Q, 1))).astype(np.float32),
        "gout": (n((E, Q)) * 1 / np.sqrt(E) * fe[:, None]).astype(np.float32),
        "vals_words": valsp[0],
        "vals_scales": valsp[1],
        "size": (np.random.uniform(0.5, 2.0, (1, I))).astype(np.float32),
        "dquery": (n((D, Q)) * 1.0 / np.sqrt(D) * fd[:, None]).astype(np.float32),
        "base": (0.5 * n((Q, T))).astype(np.float32),
        "offs": striped(idx),
    }


def reference(query, query2, keys_words, keys_scales, th, gout, vals_words, vals_scales, size, dquery, base, offs):
    idx = unstriped(offs)
    keysu = unpack_weight(keys_words, keys_scales, "e4m3")
    valsu = unpack_weight(vals_words, vals_scales, "e4m3")
    queryq = mxq(f64(query), 0, "e4m3")
    keysidxg = keysu[:, idx]
    a = queryq.T @ keysidxg
    dqueryq = mxq(f64(dquery), 0, "e4m3")
    ta = dqueryq.T @ keysidxg
    query2q = mxq(f64(query2), 0, "e4m3")
    b = query2q.T @ keysidxg
    ua = sigmoid(a - f64(th))
    ub = sigmoid(b - f64(th))
    p = 1.0 - (1.0 - ua) * (1.0 - ub)
    z = np.sum(p, axis=1, keepdims=True)
    goutq = mxq(f64(gout), 0, "e4m3")
    valsidxg = valsu[:, idx]
    c0 = goutq.T @ valsidxg
    dz = np.sum(c0 * p * f64(size) / np.square(z) * (-1.0), axis=1, keepdims=True)
    dp = c0 / z * f64(size) + dz
    dua = dp * (-1.0) * (1.0 - ub) * (-1.0)
    tua = ta * ua * (1.0 - ua)
    tp = tua * (-1.0) * (1.0 - ub) * (-1.0)
    tz = np.sum(tp, axis=1, keepdims=True)
    tdz = np.sum((tp * f64(size) * c0 - tz * z * 2.0 * c0 * p * f64(size) / np.square(z)) / np.square(z) * (-1.0), axis=1, keepdims=True)
    tdp = tz * c0 / np.square(z) * (-1.0) * f64(size) + tdz
    tdua = tdp * (-1.0) * (1.0 - ub) * (-1.0)
    tda = (tdua * ua + tua * dua) * (1.0 - ua) + tua * (-1.0) * dua * ua
    gs = tda * 512.0
    gf = np.zeros((Q, T))
    gf[:, idx] = gs
    y = f64(base) + gf
    return y

@@ -1,0 +1,218 @@
+from contextlib import ExitStack
+
+import concourse.mybir as mybir
+from concourse.masks import make_identity
+
+D, T, I, Q = 512, 2048, 512, 128
+FLOPS = 4 * 2 * D * I * Q
+
+F32 = mybir.dt.float32
+BF16 = mybir.dt.bfloat16
+I32 = mybir.dt.int32
+U32 = mybir.dt.uint32
+U16 = mybir.dt.uint16
+U8 = mybir.dt.uint8
+FP8X4 = mybir.dt.float8_e4m3fn_x4
+ALU = mybir.AluOpType
+ACT = mybir.ActivationFunctionType
+
+P = 128
+PACK = 4
+SLOT_TILES = I // P
+OUT_WIDTHS = (256, 512, 512, 512, 256)
+
+
+def tile_attend_hveitherquestion_s_kernel(
+    tc, query, query2, keys_words, keys_scales, th, gout, vals_words, vals_scales, size, dquery, base, offs, out
+):
+    nc = tc.nc
+    with ExitStack() as ctx:
+        sb = ctx.enter_context(tc.tile_pool(name="sb", bufs=1))
+        ps = ctx.enter_context(tc.psum_pool(name="ps", bufs=1))
+
+        def load_words(name, words, queue, tag):
+            pool_words = sb.tile([P, T], U32, name=name, tag=tag)
+            queue.dma_start(
+                out=pool_words[:].bitcast(I32), in_=words[0].rearrange("p n t -> p (n t)").bitcast(I32)
+            )
+            return pool_words
+
+        def zeroed_plane(name, tag):
+            plane = sb.tile([P, T], U8, name=name, tag=tag)
+            nc.vector.memset(plane[:].bitcast(I32), 0)
+            return plane
+
+        def load_scales(plane, scales, row0, queue):
+            for quad in range(4):
+                first = 32 * quad + row0
+                queue.dma_start(
+                    out=plane[first : first + 4, :].bitcast(I32),
+                    in_=scales[0, 4 * quad : 4 * quad + 4, :].bitcast(I32),
+                )
+
+        def load_rows(name, rows, tag):
+            raw = sb.tile([P, PACK, Q], F32, name=name, tag=tag)
+            nc.sync.dma_start(out=raw[:], in_=rows.rearrange("(p j) w -> p j w", j=PACK))
+            return raw
+
+        def interleave(name, raw):
+            grouped = sb.tile([P, Q, PACK], BF16, name=name, align_bytes=64)
+            nc.scalar.copy(
+                out=grouped[:].rearrange("p (c i) t -> p c t i", i=4),
+                in_=raw[:].rearrange("p t (c i) -> p c t i", i=4),
+            )
+            return grouped
+
+        def quantize(name, grouped):
+            codes = sb.tile([P, Q], U32, name=name + "_codes", align_bytes=64)
+            plane = sb.tile([P, Q], U8, name=name + "_plane", align_bytes=64)
+            nc.vector.quantize_mx(
+                out=codes[:].bitcast(FP8X4), scales=plane[:], in_=grouped[:].rearrange("p w j -> p (w j)")
+            )
+            return codes, plane
+
+        def gather(name, window, dtype):
+            picked = sb.tile([P, I], dtype, name=name, align_bytes=64)
+            nc.vector.tensor_copy(out=picked[:], in_=window[:].indirect(offsets[:]))
+            return picked
+
+        def scores(name, rows_mx):
+            bank = ps.tile([P, I], F32, name=name)
+            nc.tensor.matmul_mx(
+                out=bank[:],
+                lhsT=rows_mx[0][:].bitcast(FP8X4),
+                lhsT_scale=rows_mx[1][:],
+                rhs=key_codes[:].bitcast(FP8X4),
+                rhs_scale=key_plane[:],
+                start=True,
+                stop=True,
+            )
+            return bank
+
+        def wide(name):
+            return sb.tile([P, I], F32, name=name)
+
+        def column(name):
+            return sb.tile([P, 1], F32, name=name)
+
+        key_scale_pool = zeroed_plane("key_scale_pool", "shared_pool")
+        offsets = sb.tile([P, I // 16], U16, name="offsets")
+        nc.sync.dma_start(offsets[:], offs)
+        key_pool = load_words("key_pool", keys_words, nc.sync, "key_pool")
+        load_scales(key_scale_pool, keys_scales, 0, nc.scalar)
+        query_raw = load_rows("query_raw", query, "raw_a")
+        query2_raw = load_rows("query2_raw", query2, "raw_b")
+        th_rows = sb.tile([P, P], F32, name="th_rows")
+        nc.vector.memset(th_rows[:], 0.0)
+        nc.scalar.dma_start(out=th_rows[0:1, :], in_=th.rearrange("q o -> o q"))
+        placed = sb.tile([P, T], F32, name="placed")
+        nc.vector.memset(placed[:], 0.0)
+        val_scale_pool = zeroed_plane("val_scale_pool", "val_scale_pool")
+        load_scales(val_scale_pool, vals_scales, 4, nc.sync)
+        size_rows = sb.tile([P, P], F32, name="size_rows")
+        nc.vector.memset(size_rows[:], 0.0)
+        nc.sync.dma_start(out=size_rows[0:SLOT_TILES, :], in_=size.rearrange("o (j p) -> (o j) p", p=P))
+
+        identity = sb.tile([P, P], F32, name="identity")
+        make_identity(nc, identity[:])
+        warm = column("warm")
+        nc.scalar.activation(warm[:], placed[:, 0:1], ACT.Sigmoid)
+        th_bank = ps.tile([P, P], F32, name="th_bank")
+        nc.tensor.transpose(th_bank[:], th_rows[:], identity[:])
+        th_col = column("th_col")
+        nc.vector.tensor_copy(th_col[:], th_bank[:, 0:1])
+        neg_th = column("neg_th")
+        nc.vector.tensor_scalar(neg_th[:], th_bank[:, 0:1], -1.0, None, ALU.mult)
+
+        key_plane = gather("key_plane", key_scale_pool, U8)
+        val_pool = load_words("val_pool", vals_words, nc.scalar, "shared_pool")
+        key_codes = gather("key_codes", key_pool, U32)
+        query_mx = quantize("query", interleave("query_bf", query_raw))
+        a_bank = scores("a_bank", query_mx)
+        query2_mx = quantize("query2", interleave("query2_bf", query2_raw))
+        b_bank = scores("b_bank", query2_mx)
+        gout_raw = load_rows("gout_raw", gout, "raw_a")
+        dquery_raw = load_rows("dquery_raw", dquery, "raw_b")
+        ua = wide("ua")
+        nc.scalar.activation(ua[:], a_bank[:], ACT.Sigmoid, bias=neg_th[:], scale=1.0)
+        rest_b = wide("rest_b")
+        nc.scalar.activation(rest_b[:], b_bank[:], ACT.Sigmoid, bias=th_col[:], scale=-1.0)
+
+        size_bank = ps.tile([P, P], F32, name="size_bank")
+        nc.tensor.transpose(size_bank[:], size_rows[:], identity[:])
+        size_cols = sb.tile([P, SLOT_TILES], F32, name="size_cols")
+        nc.scalar.copy(out=size_cols[:], in_=size_bank[:, 0:SLOT_TILES])
+
+        val_plane = gather("val_plane", val_scale_pool, U8)
+        neg_ab = wide("neg_ab")
+        nc.vector.scalar_tensor_tensor(neg_ab[:], ua[:], 1.0, rest_b[:], ALU.subtract, ALU.mult)
+        val_codes = gather("val_codes", val_pool, U32)
+        base_sb = sb.tile([P, T], F32, name="base_sb", tag="shared_pool")
+        nc.sync.dma_start(out=base_sb[:], in_=base)
+        gout_bf = interleave("gout_bf", gout_raw)
+        part = wide("part")
+        z = column("z")
+        nc.scalar.activation(part[:], neg_ab[:], ACT.Identity, bias=1.0, scale=1.0, accum_out=z[:])
+        dquery_bf = interleave("dquery_bf", dquery_raw)
+        gout_mx = quantize("gout", gout_bf)
+
+        ct_bank = ps.tile([P, SLOT_TILES, Q], F32, name="ct_bank")
+        for j in range(SLOT_TILES):
+            cols = slice(j * P, (j + 1) * P)
+            nc.tensor.matmul_mx(
+                out=ct_bank[:, j, :],
+                lhsT=val_codes[:, cols].bitcast(FP8X4),
+                lhsT_scale=val_plane[4:P, cols],
+                rhs=gout_mx[0][:].bitcast(FP8X4),
+                rhs_scale=gout_mx[1][:],
+                start=True,
+                stop=True,
+            )
+
+        neg_g = wide("neg_g")
+        nc.vector.tensor_tensor(neg_g[:], ua[:], neg_ab[:], ALU.mult)
+        dquery_mx = quantize("dquery", dquery_bf)
+        ta_bank = scores("ta_bank", dquery_mx)
+
+        ct = sb.tile([P, SLOT_TILES, Q], F32, name="ct")
+        c_bank = ps.tile([P, I], F32, name="c_bank")
+        for j in range(SLOT_TILES):
+            nc.scalar.activation(ct[:, j, :], ct_bank[:, j, :], ACT.Copy, scale=size_cols[:, j : j + 1])
+        for j in range(SLOT_TILES):
+            nc.tensor.transpose(c_bank[:, j * P : (j + 1) * P], ct[:, j, :], identity[:])
+
+        rz = column("rz")
+        nc.vector.reciprocal(rz[:], z[:])
+        half_h = wide("half_h")
+        nc.vector.scalar_tensor_tensor(half_h[:], ua[:], 0.5, ta_bank[:], ALU.subtract, ALU.mult)
+        k_tp = column("k_tp")
+        nc.vector.tensor_scalar(k_tp[:], rz[:], rz[:], -512.0, ALU.mult, ALU.mult)
+        k_h = column("k_h")
+        nc.vector.tensor_scalar(k_h[:], rz[:], 1024.0, None, ALU.mult)
+        tp_s = wide("tp_s")
+        m_s = column("m_s")
+        nc.vector.scalar_tensor_tensor(tp_s[:], ta_bank[:], k_tp[:], neg_g[:], ALU.mult, ALU.mult, accum_out=m_s[:])
+        neg_hm = wide("neg_hm")
+        nc.scalar.activation(neg_hm[:], half_h[:], ACT.Identity, bias=m_s[:], scale=k_h[:])
+
+        cp = wide("cp")
+        n = column("n")
+        nc.vector.scalar_tensor_tensor(cp[:], c_bank[:], rz[:], part[:], ALU.mult, ALU.mult, accum_out=n[:])
+        tpc = wide("tpc")
+        r_s = column("r_s")
+        nc.vector.scalar_tensor_tensor(tpc[:], c_bank[:], 1.0, tp_s[:], ALU.mult, ALU.mult, accum_out=r_s[:])
+        mn = column("mn")
+        nc.vector.tensor_tensor(mn[:], m_s[:], n[:], ALU.mult)
+        neg_x = wide("neg_x")
+        nc.vector.scalar_tensor_tensor(neg_x[:], c_bank[:], n[:], neg_hm[:], ALU.subtract, ALU.mult)
+        neg_q = wide("neg_q")
+        nc.vector.tensor_scalar(neg_q[:], neg_x[:], mn[:], r_s[:], ALU.subtract, ALU.add)
+
+        nc.vector.tensor_tensor(placed[:].indirect(offsets[:]), neg_q[:], neg_g[:], ALU.mult)
+
+        first = 0
+        for width in OUT_WIDTHS:
+            cols = slice(first, first + width)
+            nc.vector.tensor_tensor(base_sb[:, cols], base_sb[:, cols], placed[:, cols], ALU.add)
+            nc.sync.dma_start(out=out[:, cols], in_=base_sb[:, cols])
+            first = first + width

@@ -30,60 +30,55 @@ def tile_attend_hveitherquestion_s_kernel(
         sb = ctx.enter_context(tc.tile_pool(name="sb", bufs=1))
         ps = ctx.enter_context(tc.psum_pool(name="ps", bufs=1))
 
-        def load_words(name, words, queue, tag):
-            pool_words = sb.tile([P, T], U32, name=name, tag=tag)
-            queue.dma_start(
+        def load_words(name, words, tag):
+            pool_words = sb.tile([P, T], U32, name=name, tag=tag, align_bytes=64)
+            nc.sync.dma_start(
                 out=pool_words[:].bitcast(I32), in_=words[0].rearrange("p n t -> p (n t)").bitcast(I32)
             )
             return pool_words
 
-        def zeroed_plane(name, tag):
-            plane = sb.tile([P, T], U8, name=name, tag=tag)
+        def zeroed_plane(name):
+            plane = sb.tile([P, T], U8, name=name, tag=name, align_bytes=64)
             nc.vector.memset(plane[:].bitcast(I32), 0)
             return plane
 
-        def load_scales(plane, scales, row0, queue):
+        def load_scales(plane, scales, row0):
             for quad in range(4):
                 first = 32 * quad + row0
-                queue.dma_start(
+                nc.sync.dma_start(
                     out=plane[first : first + 4, :].bitcast(I32),
                     in_=scales[0, 4 * quad : 4 * quad + 4, :].bitcast(I32),
                 )
 
-        def load_rows(name, rows, tag):
-            raw = sb.tile([P, PACK, Q], F32, name=name, tag=tag)
-            nc.sync.dma_start(out=raw[:], in_=rows.rearrange("(p j) w -> p j w", j=PACK))
-            return raw
+        def load_rows(raw, rows):
+            nc.sync.dma_start(out=raw, in_=rows.rearrange("(p j) w -> p j w", j=PACK))
 
-        def interleave(name, raw):
-            grouped = sb.tile([P, Q, PACK], BF16, name=name, align_bytes=64)
+        def interleave(grouped, raw):
             nc.scalar.copy(
-                out=grouped[:].rearrange("p (c i) t -> p c t i", i=4),
-                in_=raw[:].rearrange("p t (c i) -> p c t i", i=4),
+                out=grouped.rearrange("p (c i) t -> p c t i", i=4), in_=raw.rearrange("p t (c i) -> p c t i", i=4)
             )
-            return grouped
 
-        def quantize(name, grouped):
-            codes = sb.tile([P, Q], U32, name=name + "_codes", align_bytes=64)
-            plane = sb.tile([P, Q], U8, name=name + "_plane", align_bytes=64)
+        def quantize(name, grouped, width):
+            codes = sb.tile([P, width], U32, name=name + "_codes", align_bytes=64)
+            plane = sb.tile([P, width], U8, name=name + "_plane", align_bytes=64)
             nc.vector.quantize_mx(
                 out=codes[:].bitcast(FP8X4), scales=plane[:], in_=grouped[:].rearrange("p w j -> p (w j)")
             )
-            return codes, plane
+            return [(codes[:, first : first + Q], plane[:, first : first + Q]) for first in range(0, width, Q)]
 
-        def gather(name, window, dtype):
-            picked = sb.tile([P, I], dtype, name=name, align_bytes=64)
+        def gather(name, window, dtype, tag):
+            picked = sb.tile([P, I], dtype, name=name, tag=tag, align_bytes=64)
             nc.vector.tensor_copy(out=picked[:], in_=window[:].indirect(offsets[:]))
             return picked
 
-        def scores(name, rows_mx):
-            bank = ps.tile([P, I], F32, name=name)
+        def scores(name, rows_mx, codes, plane):
+            bank = ps.tile([P, codes.shape[1]], F32, name=name, tag=name)
             nc.tensor.matmul_mx(
                 out=bank[:],
-                lhsT=rows_mx[0][:].bitcast(FP8X4),
-                lhsT_scale=rows_mx[1][:],
-                rhs=key_codes[:].bitcast(FP8X4),
-                rhs_scale=key_plane[:],
+                lhsT=rows_mx[0].bitcast(FP8X4),
+                lhsT_scale=rows_mx[1],
+                rhs=codes.bitcast(FP8X4),
+                rhs_scale=plane,
                 start=True,
                 stop=True,
             )
@@ -95,120 +90,131 @@ def tile_attend_hveitherquestion_s_kernel(
         def column(name):
             return sb.tile([P, 1], F32, name=name)
 
-        key_scale_pool = zeroed_plane("key_scale_pool", "shared_pool")
         offsets = sb.tile([P, I // 16], U16, name="offsets")
         nc.sync.dma_start(offsets[:], offs)
-        key_pool = load_words("key_pool", keys_words, nc.sync, "key_pool")
-        load_scales(key_scale_pool, keys_scales, 0, nc.scalar)
-        query_raw = load_rows("query_raw", query, "raw_a")
-        query2_raw = load_rows("query2_raw", query2, "raw_b")
-        th_rows = sb.tile([P, P], F32, name="th_rows")
-        nc.vector.memset(th_rows[:], 0.0)
-        nc.scalar.dma_start(out=th_rows[0:1, :], in_=th.rearrange("q o -> o q"))
+        query_raw = sb.tile([P, PACK, Q], F32, name="query_raw")
+        load_rows(query_raw[:], query)
+        query2_raw = sb.tile([P, PACK, Q], F32, name="query2_raw", tag="query2_raw")
+        load_rows(query2_raw[:], query2)
+
+        warm_in = sb.tile([P, 1], F32, name="warm_in", tag="key_pool", align_bytes=64)
+        nc.vector.memset(warm_in[:], 0.0)
+        key_scale_pool = zeroed_plane("key_scale_pool")
+        load_scales(key_scale_pool, keys_scales, 0)
+        warm = sb.tile([P, 1], F32, name="warm", tag="dquery_raw")
+        nc.scalar.activation(warm[:], warm_in[:], ACT.Sigmoid)
+        key_pool = load_words("key_pool", keys_words, "key_pool")
+        dquery_raw = sb.tile([P, PACK, Q], F32, name="dquery_raw", tag="dquery_raw")
+        load_rows(dquery_raw[:], dquery)
+
         placed = sb.tile([P, T], F32, name="placed")
         nc.vector.memset(placed[:], 0.0)
-        val_scale_pool = zeroed_plane("val_scale_pool", "val_scale_pool")
-        load_scales(val_scale_pool, vals_scales, 4, nc.sync)
-        size_rows = sb.tile([P, P], F32, name="size_rows")
-        nc.vector.memset(size_rows[:], 0.0)
-        nc.sync.dma_start(out=size_rows[0:SLOT_TILES, :], in_=size.rearrange("o (j p) -> (o j) p", p=P))
+        val_scale_pool = zeroed_plane("val_scale_pool")
+        load_scales(val_scale_pool, vals_scales, 4)
 
+        th_col = sb.tile([P, 1], F32, name="th_col", tag="th_col", align_bytes=64)
+        nc.gpsimd.dma_start(out=th_col[:], in_=th)
         identity = sb.tile([P, P], F32, name="identity")
         make_identity(nc, identity[:])
-        warm = column("warm")
-        nc.scalar.activation(warm[:], placed[:, 0:1], ACT.Sigmoid)
-        th_bank = ps.tile([P, P], F32, name="th_bank")
-        nc.tensor.transpose(th_bank[:], th_rows[:], identity[:])
-        th_col = column("th_col")
-        nc.vector.tensor_copy(th_col[:], th_bank[:, 0:1])
-        neg_th = column("neg_th")
-        nc.vector.tensor_scalar(neg_th[:], th_bank[:, 0:1], -1.0, None, ALU.mult)
+        size_quarters = sb.tile([P, P], F32, name="size_quarters")
+        nc.gpsimd.memset(size_quarters[:], 0.0)
+        nc.gpsimd.dma_start(out=size_quarters[0:SLOT_TILES, :], in_=size.rearrange("o (j p) -> (o j) p", p=P))
 
-        key_plane = gather("key_plane", key_scale_pool, U8)
-        val_pool = load_words("val_pool", vals_words, nc.scalar, "shared_pool")
-        key_codes = gather("key_codes", key_pool, U32)
-        query_mx = quantize("query", interleave("query_bf", query_raw))
-        a_bank = scores("a_bank", query_mx)
-        query2_mx = quantize("query2", interleave("query2_bf", query2_raw))
-        b_bank = scores("b_bank", query2_mx)
-        gout_raw = load_rows("gout_raw", gout, "raw_a")
-        dquery_raw = load_rows("dquery_raw", dquery, "raw_b")
-        ua = wide("ua")
-        nc.scalar.activation(ua[:], a_bank[:], ACT.Sigmoid, bias=neg_th[:], scale=1.0)
-        rest_b = wide("rest_b")
-        nc.scalar.activation(rest_b[:], b_bank[:], ACT.Sigmoid, bias=th_col[:], scale=-1.0)
+        key_plane = gather("key_plane", key_scale_pool, U8, "key_plane")
+        early_bf = sb.tile([P, 2 * Q, PACK], BF16, name="early_bf", tag="early_bf", align_bytes=64)
+        interleave(early_bf[:, 0:Q, :], query_raw[:])
+        interleave(early_bf[:, Q : 2 * Q, :], query2_raw[:])
+        gout_raw = sb.tile([P, PACK, Q], F32, name="gout_raw", tag="query2_raw")
+        load_rows(gout_raw[:], gout)
+        val_pool = load_words("val_pool", vals_words, "key_scale_pool")
+        dquery_bf = sb.tile([P, Q, PACK], BF16, name="dquery_bf", align_bytes=64)
+        interleave(dquery_bf[:], dquery_raw[:])
+        query_mx, query2_mx = quantize("early", early_bf, 2 * Q)
+        neg_th = sb.tile([P, 1], F32, name="neg_th", tag="early_bf", align_bytes=64)
+        nc.vector.tensor_scalar(neg_th[:], th_col[:], -1.0, None, ALU.mult)
 
-        size_bank = ps.tile([P, P], F32, name="size_bank")
-        nc.tensor.transpose(size_bank[:], size_rows[:], identity[:])
-        size_cols = sb.tile([P, SLOT_TILES], F32, name="size_cols")
-        nc.scalar.copy(out=size_cols[:], in_=size_bank[:, 0:SLOT_TILES])
+        key_codes = sb.tile([P, I], U32, name="key_codes", align_bytes=64)
+        ua = sb.tile([P, I], F32, name="ua", tag="dquery_raw")
+        rest_b = sb.tile([P, I], F32, name="rest_b", tag="rest_b", align_bytes=64)
+        for half in range(2):
+            cols = slice(half * I // 2, (half + 1) * I // 2)
+            listed = offsets[:, half * I // 32 : (half + 1) * I // 32]
+            nc.vector.tensor_copy(out=key_codes[:, cols], in_=key_pool[:].indirect(listed))
+            a_bank = scores("a_bank%d" % half, query_mx, key_codes[:, cols], key_plane[:, cols])
+            b_bank = scores("b_bank%d" % half, query2_mx, key_codes[:, cols], key_plane[:, cols])
+            nc.scalar.activation(ua[:, cols], a_bank[:], ACT.Sigmoid, bias=neg_th[:], scale=1.0)
+            nc.scalar.activation(rest_b[:, cols], b_bank[:], ACT.Sigmoid, bias=th_col[:], scale=-1.0)
 
-        val_plane = gather("val_plane", val_scale_pool, U8)
-        neg_ab = wide("neg_ab")
+        val_plane = gather("val_plane", val_scale_pool, U8, "key_pool")
+        (dquery_mx,) = quantize("dquery", dquery_bf, Q)
+        ta_bank = scores("ta_bank", dquery_mx, key_codes[:], key_plane[:])
+
+        gout_bf = sb.tile([P, Q, PACK], BF16, name="gout_bf", tag="th_col", align_bytes=64)
+        interleave(gout_bf[:], gout_raw[:])
+        neg_ab = sb.tile([P, I], F32, name="neg_ab", tag="val_scale_pool", align_bytes=64)
         nc.vector.scalar_tensor_tensor(neg_ab[:], ua[:], 1.0, rest_b[:], ALU.subtract, ALU.mult)
-        val_codes = gather("val_codes", val_pool, U32)
-        base_sb = sb.tile([P, T], F32, name="base_sb", tag="shared_pool")
-        nc.sync.dma_start(out=base_sb[:], in_=base)
-        gout_bf = interleave("gout_bf", gout_raw)
+        (gout_mx,) = quantize("gout", gout_bf, Q)
+        val_codes = gather("val_codes", val_pool, U32, "rest_b")
         part = wide("part")
         z = column("z")
         nc.scalar.activation(part[:], neg_ab[:], ACT.Identity, bias=1.0, scale=1.0, accum_out=z[:])
-        dquery_bf = interleave("dquery_bf", dquery_raw)
-        gout_mx = quantize("gout", gout_bf)
+        half_g = sb.tile([P, I], F32, name="half_g", tag="key_scale_pool", align_bytes=64)
+        nc.vector.scalar_tensor_tensor(half_g[:], neg_ab[:], -0.5, ua[:], ALU.mult, ALU.mult)
+        rz = column("rz")
+        nc.vector.reciprocal(rz[:], z[:])
+        k_h = column("k_h")
+        nc.scalar.activation(k_h[:], rz[:], ACT.Copy, scale=-2048.0)
+        k_tp = column("k_tp")
+        nc.scalar.activation(k_tp[:], rz[:], ACT.Copy, scale=k_h[:])
 
-        ct_bank = ps.tile([P, SLOT_TILES, Q], F32, name="ct_bank")
+        turned = ps.tile([P, P], F32, name="turned", tag="b_bank1")
+        nc.tensor.transpose(turned[:], size_quarters[:], identity[:])
+        size_cols = sb.tile([P, SLOT_TILES], F32, name="size_cols")
+        nc.scalar.copy(out=size_cols[:], in_=turned[:, 0:SLOT_TILES])
+
+        ct = sb.tile([P, SLOT_TILES, Q], F32, name="ct", tag="ct")
+        ct_banks = [ps.tile([P, 2, Q], F32, name="ct_bank%d" % u, tag=tag) for u, tag in enumerate(("a_bank0", "b_bank0"))]
         for j in range(SLOT_TILES):
             cols = slice(j * P, (j + 1) * P)
             nc.tensor.matmul_mx(
-                out=ct_bank[:, j, :],
+                out=ct_banks[j // 2][:, j % 2, :],
                 lhsT=val_codes[:, cols].bitcast(FP8X4),
                 lhsT_scale=val_plane[4:P, cols],
-                rhs=gout_mx[0][:].bitcast(FP8X4),
-                rhs_scale=gout_mx[1][:],
+                rhs=gout_mx[0].bitcast(FP8X4),
+                rhs_scale=gout_mx[1],
                 start=True,
                 stop=True,
             )
-
-        neg_g = wide("neg_g")
-        nc.vector.tensor_tensor(neg_g[:], ua[:], neg_ab[:], ALU.mult)
-        dquery_mx = quantize("dquery", dquery_bf)
-        ta_bank = scores("ta_bank", dquery_mx)
-
-        ct = sb.tile([P, SLOT_TILES, Q], F32, name="ct")
-        c_bank = ps.tile([P, I], F32, name="c_bank")
+        base_sb = sb.tile([P, T], F32, name="base_sb", tag="key_pool", align_bytes=64)
+        nc.sync.dma_start(out=base_sb[:], in_=base)
         for j in range(SLOT_TILES):
-            nc.scalar.activation(ct[:, j, :], ct_bank[:, j, :], ACT.Copy, scale=size_cols[:, j : j + 1])
+            nc.scalar.activation(ct[:, j, :], ct_banks[j // 2][:, j % 2, :], ACT.Copy, scale=size_cols[:, j : j + 1])
+        c = ps.tile([P, I], F32, name="c")
         for j in range(SLOT_TILES):
-            nc.tensor.transpose(c_bank[:, j * P : (j + 1) * P], ct[:, j, :], identity[:])
+            nc.tensor.transpose(c[:, j * P : (j + 1) * P], ct[:, j, :], identity[:])
 
-        rz = column("rz")
-        nc.vector.reciprocal(rz[:], z[:])
-        half_h = wide("half_h")
+        half_h = sb.tile([P, I], F32, name="half_h", tag="val_scale_pool", align_bytes=64)
         nc.vector.scalar_tensor_tensor(half_h[:], ua[:], 0.5, ta_bank[:], ALU.subtract, ALU.mult)
-        k_tp = column("k_tp")
-        nc.vector.tensor_scalar(k_tp[:], rz[:], rz[:], -512.0, ALU.mult, ALU.mult)
-        k_h = column("k_h")
-        nc.vector.tensor_scalar(k_h[:], rz[:], 1024.0, None, ALU.mult)
         tp_s = wide("tp_s")
         m_s = column("m_s")
-        nc.vector.scalar_tensor_tensor(tp_s[:], ta_bank[:], k_tp[:], neg_g[:], ALU.mult, ALU.mult, accum_out=m_s[:])
-        neg_hm = wide("neg_hm")
-        nc.scalar.activation(neg_hm[:], half_h[:], ACT.Identity, bias=m_s[:], scale=k_h[:])
+        nc.vector.scalar_tensor_tensor(tp_s[:], ta_bank[:], k_tp[:], half_g[:], ALU.mult, ALU.mult, accum_out=m_s[:])
+        hm = sb.tile([P, I], F32, name="hm", tag="ct")
+        nc.scalar.activation(hm[:], half_h[:], ACT.Identity, bias=m_s[:], scale=k_h[:])
 
         cp = wide("cp")
         n = column("n")
-        nc.vector.scalar_tensor_tensor(cp[:], c_bank[:], rz[:], part[:], ALU.mult, ALU.mult, accum_out=n[:])
+        nc.vector.scalar_tensor_tensor(cp[:], c[:], rz[:], part[:], ALU.mult, ALU.mult, accum_out=n[:])
+        mn = column("mn")
+        nc.scalar.activation(mn[:], m_s[:], ACT.Copy, scale=n[:])
         tpc = wide("tpc")
         r_s = column("r_s")
-        nc.vector.scalar_tensor_tensor(tpc[:], c_bank[:], 1.0, tp_s[:], ALU.mult, ALU.mult, accum_out=r_s[:])
-        mn = column("mn")
-        nc.vector.tensor_tensor(mn[:], m_s[:], n[:], ALU.mult)
-        neg_x = wide("neg_x")
-        nc.vector.scalar_tensor_tensor(neg_x[:], c_bank[:], n[:], neg_hm[:], ALU.subtract, ALU.mult)
-        neg_q = wide("neg_q")
-        nc.vector.tensor_scalar(neg_q[:], neg_x[:], mn[:], r_s[:], ALU.subtract, ALU.add)
+        nc.vector.scalar_tensor_tensor(tpc[:], c[:], 1.0, tp_s[:], ALU.mult, ALU.mult, accum_out=r_s[:])
+        x = wide("x")
+        nc.vector.scalar_tensor_tensor(x[:], c[:], n[:], hm[:], ALU.subtract, ALU.mult)
+        factor = wide("factor")
+        nc.vector.tensor_scalar(factor[:], x[:], mn[:], r_s[:], ALU.subtract, ALU.add)
 
-        nc.vector.tensor_tensor(placed[:].indirect(offsets[:]), neg_q[:], neg_g[:], ALU.mult)
+        nc.vector.tensor_tensor(placed[:].indirect(offsets[:]), factor[:], half_g[:], ALU.mult)
 
         first = 0
         for width in OUT_WIDTHS:

from contextlib import ExitStack

import concourse.mybir as mybir
from concourse.masks import make_identity

D, T, I, Q = 512, 2048, 512, 128
FLOPS = 4 * 2 * D * I * Q

F32 = mybir.dt.float32
BF16 = mybir.dt.bfloat16
I32 = mybir.dt.int32
U32 = mybir.dt.uint32
U16 = mybir.dt.uint16
U8 = mybir.dt.uint8
FP8X4 = mybir.dt.float8_e4m3fn_x4
ALU = mybir.AluOpType
ACT = mybir.ActivationFunctionType

P = 128
PACK = 4
SLOT_TILES = I // P
OUT_WIDTHS = (256, 512, 512, 512, 256)


def tile_attend_hveitherquestion_s_kernel(
    tc, query, query2, keys_words, keys_scales, th, gout, vals_words, vals_scales, size, dquery, base, offs, out
):
    nc = tc.nc
    with ExitStack() as ctx:
        sb = ctx.enter_context(tc.tile_pool(name="sb", bufs=1))
        ps = ctx.enter_context(tc.psum_pool(name="ps", bufs=1))

        def load_words(name, words, tag):
            pool_words = sb.tile([P, T], U32, name=name, tag=tag, align_bytes=64)
            nc.sync.dma_start(
                out=pool_words[:].bitcast(I32), in_=words[0].rearrange("p n t -> p (n t)").bitcast(I32)
            )
            return pool_words

        def zeroed_plane(name):
            plane = sb.tile([P, T], U8, name=name, tag=name, align_bytes=64)
            nc.vector.memset(plane[:].bitcast(I32), 0)
            return plane

        def load_scales(plane, scales, row0):
            for quad in range(4):
                first = 32 * quad + row0
                nc.sync.dma_start(
                    out=plane[first : first + 4, :].bitcast(I32),
                    in_=scales[0, 4 * quad : 4 * quad + 4, :].bitcast(I32),
                )

        def load_rows(raw, rows):
            nc.sync.dma_start(out=raw, in_=rows.rearrange("(p j) w -> p j w", j=PACK))

        def interleave(grouped, raw):
            nc.scalar.copy(
                out=grouped.rearrange("p (c i) t -> p c t i", i=4), in_=raw.rearrange("p t (c i) -> p c t i", i=4)
            )

        def quantize(name, grouped, width):
            codes = sb.tile([P, width], U32, name=name + "_codes", align_bytes=64)
            plane = sb.tile([P, width], U8, name=name + "_plane", align_bytes=64)
            nc.vector.quantize_mx(
                out=codes[:].bitcast(FP8X4), scales=plane[:], in_=grouped[:].rearrange("p w j -> p (w j)")
            )
            return [(codes[:, first : first + Q], plane[:, first : first + Q]) for first in range(0, width, Q)]

        def gather(name, window, dtype, tag):
            picked = sb.tile([P, I], dtype, name=name, tag=tag, align_bytes=64)
            nc.vector.tensor_copy(out=picked[:], in_=window[:].indirect(offsets[:]))
            return picked

        def scores(name, rows_mx, codes, plane):
            bank = ps.tile([P, codes.shape[1]], F32, name=name, tag=name)
            nc.tensor.matmul_mx(
                out=bank[:],
                lhsT=rows_mx[0].bitcast(FP8X4),
                lhsT_scale=rows_mx[1],
                rhs=codes.bitcast(FP8X4),
                rhs_scale=plane,
                start=True,
                stop=True,
            )
            return bank

        def wide(name):
            return sb.tile([P, I], F32, name=name)

        def column(name):
            return sb.tile([P, 1], F32, name=name)

        offsets = sb.tile([P, I // 16], U16, name="offsets")
        nc.sync.dma_start(offsets[:], offs)
        query_raw = sb.tile([P, PACK, Q], F32, name="query_raw")
        load_rows(query_raw[:], query)
        query2_raw = sb.tile([P, PACK, Q], F32, name="query2_raw", tag="query2_raw")
        load_rows(query2_raw[:], query2)

        warm_in = sb.tile([P, 1], F32, name="warm_in", tag="key_pool", align_bytes=64)
        nc.vector.memset(warm_in[:], 0.0)
        key_scale_pool = zeroed_plane("key_scale_pool")
        load_scales(key_scale_pool, keys_scales, 0)
        warm = sb.tile([P, 1], F32, name="warm", tag="dquery_raw")
        nc.scalar.activation(warm[:], warm_in[:], ACT.Sigmoid)
        key_pool = load_words("key_pool", keys_words, "key_pool")
        dquery_raw = sb.tile([P, PACK, Q], F32, name="dquery_raw", tag="dquery_raw")
        load_rows(dquery_raw[:], dquery)

        placed = sb.tile([P, T], F32, name="placed")
        nc.vector.memset(placed[:], 0.0)
        val_scale_pool = zeroed_plane("val_scale_pool")
        load_scales(val_scale_pool, vals_scales, 4)

        th_col = sb.tile([P, 1], F32, name="th_col", tag="th_col", align_bytes=64)
        nc.gpsimd.dma_start(out=th_col[:], in_=th)
        identity = sb.tile([P, P], F32, name="identity")
        make_identity(nc, identity[:])
        size_quarters = sb.tile([P, P], F32, name="size_quarters")
        nc.gpsimd.memset(size_quarters[:], 0.0)
        nc.gpsimd.dma_start(out=size_quarters[0:SLOT_TILES, :], in_=size.rearrange("o (j p) -> (o j) p", p=P))

        key_plane = gather("key_plane", key_scale_pool, U8, "key_plane")
        early_bf = sb.tile([P, 2 * Q, PACK], BF16, name="early_bf", tag="early_bf", align_bytes=64)
        interleave(early_bf[:, 0:Q, :], query_raw[:])
        interleave(early_bf[:, Q : 2 * Q, :], query2_raw[:])
        gout_raw = sb.tile([P, PACK, Q], F32, name="gout_raw", tag="query2_raw")
        load_rows(gout_raw[:], gout)
        val_pool = load_words("val_pool", vals_words, "key_scale_pool")
        dquery_bf = sb.tile([P, Q, PACK], BF16, name="dquery_bf", align_bytes=64)
        interleave(dquery_bf[:], dquery_raw[:])
        query_mx, query2_mx = quantize("early", early_bf, 2 * Q)
        neg_th = sb.tile([P, 1], F32, name="neg_th", tag="early_bf", align_bytes=64)
        nc.vector.tensor_scalar(neg_th[:], th_col[:], -1.0, None, ALU.mult)

        key_codes = sb.tile([P, I], U32, name="key_codes", align_bytes=64)
        ua = sb.tile([P, I], F32, name="ua", tag="dquery_raw")
        rest_b = sb.tile([P, I], F32, name="rest_b", tag="rest_b", align_bytes=64)
        for half in range(2):
            cols = slice(half * I // 2, (half + 1) * I // 2)
            listed = offsets[:, half * I // 32 : (half + 1) * I // 32]
            nc.vector.tensor_copy(out=key_codes[:, cols], in_=key_pool[:].indirect(listed))
            a_bank = scores("a_bank%d" % half, query_mx, key_codes[:, cols], key_plane[:, cols])
            b_bank = scores("b_bank%d" % half, query2_mx, key_codes[:, cols], key_plane[:, cols])
            nc.scalar.activation(ua[:, cols], a_bank[:], ACT.Sigmoid, bias=neg_th[:], scale=1.0)
            nc.scalar.activation(rest_b[:, cols], b_bank[:], ACT.Sigmoid, bias=th_col[:], scale=-1.0)

        val_plane = gather("val_plane", val_scale_pool, U8, "key_pool")
        (dquery_mx,) = quantize("dquery", dquery_bf, Q)
        ta_bank = scores("ta_bank", dquery_mx, key_codes[:], key_plane[:])

        gout_bf = sb.tile([P, Q, PACK], BF16, name="gout_bf", tag="th_col", align_bytes=64)
        interleave(gout_bf[:], gout_raw[:])
        neg_ab = sb.tile([P, I], F32, name="neg_ab", tag="val_scale_pool", align_bytes=64)
        nc.vector.scalar_tensor_tensor(neg_ab[:], ua[:], 1.0, rest_b[:], ALU.subtract, ALU.mult)
        (gout_mx,) = quantize("gout", gout_bf, Q)
        val_codes = gather("val_codes", val_pool, U32, "rest_b")
        part = wide("part")
        z = column("z")
        nc.scalar.activation(part[:], neg_ab[:], ACT.Identity, bias=1.0, scale=1.0, accum_out=z[:])
        half_g = sb.tile([P, I], F32, name="half_g", tag="key_scale_pool", align_bytes=64)
        nc.vector.scalar_tensor_tensor(half_g[:], neg_ab[:], -0.5, ua[:], ALU.mult, ALU.mult)
        rz = column("rz")
        nc.vector.reciprocal(rz[:], z[:])
        k_h = column("k_h")
        nc.scalar.activation(k_h[:], rz[:], ACT.Copy, scale=-2048.0)
        k_tp = column("k_tp")
        nc.scalar.activation(k_tp[:], rz[:], ACT.Copy, scale=k_h[:])

        turned = ps.tile([P, P], F32, name="turned", tag="b_bank1")
        nc.tensor.transpose(turned[:], size_quarters[:], identity[:])
        size_cols = sb.tile([P, SLOT_TILES], F32, name="size_cols")
        nc.scalar.copy(out=size_cols[:], in_=turned[:, 0:SLOT_TILES])

        ct = sb.tile([P, SLOT_TILES, Q], F32, name="ct", tag="ct")
        ct_banks = [ps.tile([P, 2, Q], F32, name="ct_bank%d" % u, tag=tag) for u, tag in enumerate(("a_bank0", "b_bank0"))]
        for j in range(SLOT_TILES):
            cols = slice(j * P, (j + 1) * P)
            nc.tensor.matmul_mx(
                out=ct_banks[j // 2][:, j % 2, :],
                lhsT=val_codes[:, cols].bitcast(FP8X4),
                lhsT_scale=val_plane[4:P, cols],
                rhs=gout_mx[0].bitcast(FP8X4),
                rhs_scale=gout_mx[1],
                start=True,
                stop=True,
            )
        base_sb = sb.tile([P, T], F32, name="base_sb", tag="key_pool", align_bytes=64)
        nc.sync.dma_start(out=base_sb[:], in_=base)
        for j in range(SLOT_TILES):
            nc.scalar.activation(ct[:, j, :], ct_banks[j // 2][:, j % 2, :], ACT.Copy, scale=size_cols[:, j : j + 1])
        c = ps.tile([P, I], F32, name="c")
        for j in range(SLOT_TILES):
            nc.tensor.transpose(c[:, j * P : (j + 1) * P], ct[:, j, :], identity[:])

        half_h = sb.tile([P, I], F32, name="half_h", tag="val_scale_pool", align_bytes=64)
        nc.vector.scalar_tensor_tensor(half_h[:], ua[:], 0.5, ta_bank[:], ALU.subtract, ALU.mult)
        tp_s = wide("tp_s")
        m_s = column("m_s")
        nc.vector.scalar_tensor_tensor(tp_s[:], ta_bank[:], k_tp[:], half_g[:], ALU.mult, ALU.mult, accum_out=m_s[:])
        hm = sb.tile([P, I], F32, name="hm", tag="ct")
        nc.scalar.activation(hm[:], half_h[:], ACT.Identity, bias=m_s[:], scale=k_h[:])

        cp = wide("cp")
        n = column("n")
        nc.vector.scalar_tensor_tensor(cp[:], c[:], rz[:], part[:], ALU.mult, ALU.mult, accum_out=n[:])
        mn = column("mn")
        nc.scalar.activation(mn[:], m_s[:], ACT.Copy, scale=n[:])
        tpc = wide("tpc")
        r_s = column("r_s")
        nc.vector.scalar_tensor_tensor(tpc[:], c[:], 1.0, tp_s[:], ALU.mult, ALU.mult, accum_out=r_s[:])
        x = wide("x")
        nc.vector.scalar_tensor_tensor(x[:], c[:], n[:], hm[:], ALU.subtract, ALU.mult)
        factor = wide("factor")
        nc.vector.tensor_scalar(factor[:], x[:], mn[:], r_s[:], ALU.subtract, ALU.add)

        nc.vector.tensor_tensor(placed[:].indirect(offsets[:]), factor[:], half_g[:], ALU.mult)

        first = 0
        for width in OUT_WIDTHS:
            cols = slice(first, first + width)
            nc.vector.tensor_tensor(base_sb[:, cols], base_sb[:, cols], placed[:, cols], ALU.add)
            nc.sync.dma_start(out=out[:, cols], in_=base_sb[:, cols])
            first = first + width
